import numpy as np
import ml_dtypes


def mxq(x, axis, fmt="e4m3"):
    dtype, down = {"e4m3": (ml_dtypes.float8_e4m3fn, 7), "e5m2": (ml_dtypes.float8_e5m2, 14)}[fmt]
    v = np.moveaxis(np.asarray(x, np.float32).astype(ml_dtypes.bfloat16).astype(np.float64), axis, -1)
    blocks = v.reshape(v.shape[:-1] + (-1, 32))
    amax = np.abs(blocks).max(-1, keepdims=True)
    byte = np.maximum(np.where(amax > 0, np.frexp(amax)[1] - 1 + 127, 0) - down, 1)
    scale = np.exp2(byte - 127.0)
    codes = (blocks / scale).astype(np.float32).astype(dtype).astype(np.float64)
    return np.moveaxis((codes * scale).reshape(v.shape), -1, axis)


WIDE = False


def mx_kscale(k):
    if not WIDE:
        return np.ones(k)
    levels = np.array([10, -10, 5, -5, 0])
    if k % 512:
        return np.exp2(np.random.permutation(np.resize(levels, k // 32))).repeat(32)
    a = np.empty((k // 512, 16))
    for p in range(k // 512):
        a[p, :8] = np.random.permutation(np.resize(levels, 8))
        for g in range(8):
            far = levels[np.abs(levels - a[p, g]) >= 10]
            a[p, g + 8] = far[np.random.randint(len(far))]
    return np.exp2(a.ravel()).repeat(32)


def f64(x):
    return np.asarray(x).astype(np.float64)


def striped(idx):
    return np.tile(idx.reshape(-1, 16).T, (8, 1)).astype(np.uint16)


def unstriped(offs):
    return offs[:16].T.reshape(-1).astype(np.int64)


def striped8(idx):
    return np.concatenate([x.reshape(-1, 16).T for x in idx]).astype(np.uint16)


def runs(offs, k):
    lists = np.stack([offs[16 * r : 16 * r + 16].T.reshape(-1) for r in range(8)]).astype(np.int64)
    return lists[np.arange(k) % 512 // 64]


def pack_weight(w):
    k, n = w.shape
    w = f64(np.asarray(w, np.float32).astype(ml_dtypes.bfloat16)).reshape(k // 32, 32, n)
    amax = np.abs(w).max(1)
    byte = np.clip(np.where(amax > 0, np.frexp(amax)[1] - 1 + 127 - 7, 1), 1, 254)
    scaled = (w * np.exp2(127.0 - byte)[:, None, :]).reshape(k, n).astype(np.float32)
    words = np.ascontiguousarray(scaled.reshape(k // 512, 128, 4, n).transpose(0, 1, 3, 2)).astype(ml_dtypes.float8_e4m3fn).view(np.uint8)
    return words, np.ascontiguousarray(byte.astype(np.uint8).reshape(k // 512, 16, n))


def unpack_weight(words, scales):
    g, p, n, _ = words.shape
    vals = np.ascontiguousarray(words).view(ml_dtypes.float8_e4m3fn).astype(np.float64) * np.repeat(np.exp2(scales.astype(np.float64) - 127.0), 8, axis=1)[..., None]
    return vals.transpose(0, 1, 3, 2).reshape(g * 512, n)


E2M1 = np.array([0.0, 0.5, 1.0, 1.5, 2.0, 3.0, 4.0, 6.0, -0.0, -0.5, -1.0, -1.5, -2.0, -3.0, -4.0, -6.0])


def pack_fp4(w):
    k, n = w.shape
    w = f64(np.asarray(w, np.float32).astype(ml_dtypes.bfloat16)).reshape(k // 32, 32, n)
    amax = np.abs(w).max(1)
    mant, ex = np.frexp(amax / 6.0)
    byte = np.clip(np.where(amax > 0, np.where(mant > 0.5, ex, ex - 1) + 127, 1), 1, 254)
    scaled = (w * np.exp2(127.0 - byte)[:, None, :]).reshape(k, n).astype(np.float32)
    c = np.ascontiguousarray(scaled.reshape(k // 512, 128, 4, n).transpose(0, 1, 3, 2)).astype(ml_dtypes.float4_e2m1fn).view(np.uint8) & 0xF
    words = (c[..., 0::2] | (c[..., 1::2] << 4)).reshape(k // 512, 128, 2 * n)
    return np.ascontiguousarray(words), np.ascontiguousarray(byte.astype(np.uint8).reshape(k // 512, 16, n))


def unpack_fp4(words, scales):
    g, _, n = scales.shape
    words = np.ascontiguousarray(words).reshape(g, 128, n, 2)
    nib = np.empty((g, 128, n, 4), np.uint8)
    nib[..., 0::2] = words & 0xF
    nib[..., 1::2] = words >> 4
    vals = E2M1[nib] * np.repeat(np.exp2(scales.astype(np.float64) - 127.0), 8, axis=1)[..., None]
    return vals.transpose(0, 1, 3, 2).reshape(g * 512, n)


def sigmoid(v):
    return 1.0 / (1.0 + np.exp(-np.maximum(v, -700.0)))

def planes(y):
    n, m = y.shape
    v = y.astype(np.float32).astype(ml_dtypes.bfloat16).astype(np.float64).reshape(n // 32, 32, m)
    top = np.abs(v).max(1)
    byte = np.clip(np.where(top > 0, np.frexp(top)[1] - 1 + 127 - 7, 1), 1, 254)
    codes = (v * np.exp2(127.0 - byte)[:, None, :]).reshape(n, m).astype(np.float32).astype(ml_dtypes.float8_e4m3fn).view(np.uint8)
    words = codes.reshape(n // 512, 128, 4, m).transpose(0, 1, 3, 2)
    return np.ascontiguousarray(words), np.ascontiguousarray(byte.astype(np.uint8).reshape(n // 512, 16, m))


K, T, S, H, C = 512, 2048, 512, 512, 512


def setup_inputs():
    n = np.random.standard_normal
    s = mx_kscale(K)[:, None]
    packed_xT = pack_weight(n((K, T)) * s)
    packed_w1 = pack_fp4(n((K, H)) / np.sqrt(K) / s)
    return {
        "x_words": packed_xT[0],
        "x_scales": packed_xT[1],
        "w1_words": packed_w1[0],
        "w1_scales": packed_w1[1],
        "gs": (np.random.uniform(0.5, 1.5, (K, 1)) / s).astype(np.float32),
        "sl": np.random.uniform(1.0, 2.0, (C, 1)).astype(np.float32),
        "th": (0.5 * n((C, 1))).astype(np.float32),
        "sl2": np.random.uniform(1.0, 2.0, (C, 1)).astype(np.float32),
        "th2": (0.5 * n((C, 1))).astype(np.float32),
        "offs": striped8(np.random.randint(0, T, (8, S))),
        "n1": striped(np.random.permutation(S)),
        "cand": striped8(np.random.randint(0, T, (8, C))),
        "n2": striped8(np.stack([np.random.permutation(S) for _ in range(8)])),
        "n3": striped8(np.stack([np.random.permutation(S) for _ in range(8)])),
    }


def reference(x_words, x_scales, w1_words, w1_scales, gs, sl, th, sl2, th2, offs, n1, cand, n2, n3):
    x_cand = unpack_weight(x_words, x_scales)[np.arange(K)[:, None], runs(cand, K)]
    xq = unpack_weight(x_words, x_scales)[np.arange(K)[:, None], runs(offs, K)]
    y = unpack_fp4(w1_words, w1_scales).T @ xq
    st = y - y[:, unstriped(n1)]
    z = f64(gs) * (st - (0.5 * st[:, unstriped(n1)]))
    s = 0.0625 * ((x_cand.T @ mxq(z, 0, "e4m3")))
    sg = sigmoid(f64(sl) * (s[np.arange(C)[:, None], runs(n2, C)] - f64(th)))
    sg2 = sigmoid(f64(sl2) * (f64(th2) - (s[np.arange(C)[:, None], runs(n3, C)])))
    out_0 = 2.0 * ((s * sg) * sg2)
    return (out_0,) + planes(out_0)

@@ -1,0 +1,216 @@
+import concourse.mybir as mybir
+
+F32 = mybir.dt.float32
+BF16 = mybir.dt.bfloat16
+I32 = mybir.dt.int32
+U32 = mybir.dt.uint32
+U16 = mybir.dt.uint16
+U8 = mybir.dt.uint8
+FP8X4 = mybir.dt.float8_e4m3fn_x4
+FP4X4 = mybir.dt.float4_e2m1fn_x4
+MULT = mybir.AluOpType.mult
+ADD = mybir.AluOpType.add
+SUBTRACT = mybir.AluOpType.subtract
+COPY = mybir.ActivationFunctionType.Copy
+SIGMOID = mybir.ActivationFunctionType.Sigmoid
+
+P = 128
+PACK = 4
+T = 2048
+S = 512
+PER_COLUMN = 16
+FLOPS = 2 * 2 * 512 * 512 * 512
+
+HALVES = [(0, 256), (256, 512)]
+Z_CHUNKS = [(0, 128), (128, 256), (256, 384), (384, 512)]
+OUT_CHUNKS = [(0, 256), (256, 384), (384, 512)]
+SCALAR_TILES = (0, 1)
+
+
+def entries(list_tile, lo, hi):
+    return list_tile[:, lo // PER_COLUMN : hi // PER_COLUMN]
+
+
+def by_lines(planes):
+    return planes.rearrange("p t (c i) -> p c t i", i=4)
+
+
+def into_words(values):
+    return values.rearrange("p (c i t) -> p c t i", i=4, t=PACK)
+
+
+def place_scale_rows(queues, placed, gathered):
+    for i, queue in enumerate(queues):
+        queue.dma_start(out=placed[:].bitcast(I32)[i:P:32, :], in_=gathered[:].bitcast(I32)[8 * i : P : 32, :])
+
+
+def tile_picked_hcandtwiceecr_none_po_kernel(
+    tc, x_words, x_scales, w1_words, w1_scales, gs, sl, th, sl2, th2, offs, n1, cand, n2, n3, out_0, out_1, out_2
+):
+    nc = tc.nc
+    with tc.tile_pool(name="held", bufs=1) as held, tc.psum_pool(name="psum", bufs=1) as psum:
+
+        def sbuf(name, shape, dtype):
+            return held.tile(shape, dtype, name=name, align_bytes=64)
+
+        def load_list(name, dram):
+            list_tile = sbuf(name, [P, S // PER_COLUMN], U16)
+            nc.sync.dma_start(list_tile[:], dram)
+            return list_tile
+
+        def load_rows(columns, dram):
+            nc.sync.dma_start(out=columns, in_=dram.rearrange("(p t) o -> p (t o)", t=PACK))
+            return columns
+
+        table_scales = sbuf("table_scales", [P, T], U8)
+        w_scales_raw = sbuf("w_scales_raw", [P, S], U8)
+        place_scales = sbuf("place_scales", [P, S], U8)
+        nc.vector.memset(place_scales[:].bitcast(I32), 0)
+        cand_scales = sbuf("cand_scales", [P, S], U8)
+        nc.vector.memset(cand_scales[:].bitcast(I32), 0)
+
+        offs_l = load_list("offs_l", offs)
+        nc.sync.dma_start(
+            out=table_scales[:].bitcast(I32), in_=x_scales[0].bitcast(I32).unsqueeze(1).broadcast_to([16, 8, T // 4])
+        )
+        w_raw = sbuf("w_raw", [P, 2 * S], U8)
+        for q in range(4):
+            queue = nc.sync if q < 2 else nc.gpsimd
+            queue.dma_start(
+                out=w_scales_raw[:].bitcast(I32)[32 * q : 32 * (q + 1), :],
+                in_=w1_scales[0].bitcast(I32)[4 * q : 4 * q + 4, :].unsqueeze(0).broadcast_to([8, 4, S // 4]),
+            )
+        nc.sync.dma_start(out=w_raw[:].bitcast(I32), in_=w1_words[0].bitcast(I32))
+        gs_c = load_rows(sbuf("gs_c", [P, PACK], F32)[:], gs)
+        cand_l = load_list("cand_l", cand)
+        table_words = sbuf("table_words", [P, T], U32)
+        nc.sync.dma_start(out=table_words[:].bitcast(I32), in_=x_words[0].rearrange("p n t -> p (n t)").bitcast(I32))
+        n1_l = load_list("n1_l", n1)
+        n2_l = load_list("n2_l", n2)
+        n3_l = load_list("n3_l", n3)
+
+        place_bytes = sbuf("place_bytes", [P, S], U8)
+        nc.vector.tensor_copy(place_bytes[:], table_scales[:].indirect(offs_l[:]))
+        place_scale_rows((nc.scalar, nc.scalar, nc.sync, nc.sync), place_scales, place_bytes)
+
+        w_words = sbuf("w_words", [P, 2 * S], U8)
+        nc.scalar.copy(
+            w_words[:].bitcast(U16).rearrange("p (t m) -> p t m", t=PACK),
+            w_raw[:].bitcast(U16).rearrange("p (m t) -> p t m", t=PACK),
+        )
+        w_scales = sbuf("w_scales", [P, S], U8)
+        nc.vector.tensor_copy(
+            w_scales[:].rearrange("p (t m) -> p t m", t=PACK), w_scales_raw[:].rearrange("p (m t) -> p t m", t=PACK)
+        )
+
+        gate_rows = held.tile([P, 4, 8], F32, name="gate_rows", tag="w_scales_raw", align_bytes=64)
+        sl_c, th_c, sl2_c, th2_c = [load_rows(gate_rows[:, v, 0:PACK], dram) for v, dram in enumerate((sl, th, sl2, th2))]
+
+        place_words = sbuf("place_words", [P, S], U32)
+        y = [sbuf(f"y{t}", [P, S], F32) for t in range(PACK)]
+        for h, (lo, hi) in enumerate(HALVES):
+            nc.vector.tensor_copy(place_words[:, lo:hi], table_words[:].indirect(entries(offs_l, lo, hi)))
+            for t in range(PACK):
+                acc = psum.tile([P, hi - lo], F32, name=f"y_acc{h}{t}", tag=f"bank{PACK * h + t}")
+                nc.tensor.matmul_mx(
+                    out=acc[:],
+                    lhsT=w_words[:, 2 * P * t : 2 * P * (t + 1)].bitcast(FP4X4),
+                    lhsT_scale=w_scales[:, P * t : P * (t + 1)],
+                    rhs=place_words[:, lo:hi].bitcast(FP8X4),
+                    rhs_scale=place_scales[:, lo:hi],
+                    start=True,
+                    stop=True,
+                )
+                nc.scalar.activation(y[t][:, lo:hi], acc[:], COPY, scale=gs_c[:, t : t + 1])
+
+        cand_bytes = sbuf("cand_bytes", [P, S], U8)
+        nc.vector.tensor_copy(cand_bytes[:], table_scales[:].indirect(cand_l[:]))
+        cand_bytes_dealt = sbuf("cand_bytes_dealt", [P, S], U8)
+        nc.vector.tensor_copy(
+            cand_bytes_dealt[:].rearrange("p (t m) -> p t m", t=PACK),
+            cand_bytes[:].rearrange("p (m t) -> p t m", t=PACK),
+        )
+        place_scale_rows((nc.sync,) * 4, cand_scales, cand_bytes_dealt)
+        cand_picked = sbuf("cand_picked", [P, S], U32)
+        nc.vector.tensor_copy(cand_picked[:], table_words[:].indirect(cand_l[:]))
+        cand_words = sbuf("cand_words", [P, S], U32)
+        nc.vector.tensor_copy(
+            cand_words[:].bitcast(I32).rearrange("p (t m) -> p t m", t=PACK),
+            cand_picked[:].bitcast(I32).rearrange("p (m t) -> p t m", t=PACK),
+        )
+
+        st = sbuf("st", [P, PACK, S], F32)
+        for t in (0, 2, 1, 3):
+            y_at = sbuf(f"y_at{t}", [P, S], F32)
+            for lo, hi in HALVES:
+                looked_up = y[t][:].indirect(entries(n1_l, lo, hi))
+                if t in SCALAR_TILES:
+                    nc.scalar.activation(y_at[:, lo:hi], looked_up, COPY)
+                else:
+                    nc.vector.tensor_copy(y_at[:, lo:hi], looked_up)
+            nc.vector.tensor_tensor(st[:, t, :], y[t][:], y_at[:], SUBTRACT)
+
+        bias1 = sbuf("bias1", [P, PACK], F32)
+        nc.vector.scalar_tensor_tensor(bias1[:], sl_c, -1.0, th_c, MULT, MULT)
+        scale2 = sbuf("scale2", [P, PACK], F32)
+        nc.vector.tensor_scalar(scale2[:], sl2_c, -1.0, None, MULT)
+        bias2 = sbuf("bias2", [P, PACK], F32)
+        nc.vector.tensor_tensor(bias2[:], sl2_c, th2_c, MULT)
+
+        s = [sbuf(f"s{t}", [P, S], F32) for t in range(PACK)]
+        s_acc = {t: psum.tile([P, S], F32, name=f"s_acc{t}", tag=f"bank{PACK + t}") for t in range(1, PACK)}
+        for c, (lo, hi) in enumerate(Z_CHUNKS):
+            n = hi - lo
+            half_at = sbuf(f"half_at{c}", [P, PACK, n], F32)
+            for t in (0, 2, 1, 3):
+                nc.scalar.activation(half_at[:, t, :], st[:, t, :].indirect(entries(n1_l, lo, hi)), COPY, scale=0.5)
+            z = sbuf(f"z{c}", [P, PACK * n], BF16)
+            nc.vector.tensor_tensor(into_words(z[:]), by_lines(st[:, :, lo:hi]), by_lines(half_at[:]), SUBTRACT)
+            z_words = sbuf(f"z_words{c}", [P, n], U32)
+            z_scales = sbuf(f"z_scales{c}", [P, n], U8)
+            nc.vector.quantize_mx(out=z_words[:].bitcast(FP8X4), scales=z_scales[:], in_=z[:])
+            first = psum.tile([P, n], F32, name=f"s_first{c}", tag=f"bank{c}")
+            for t in range(PACK):
+                nc.tensor.matmul_mx(
+                    out=first[:] if t == 0 else s_acc[t][:, lo:hi],
+                    lhsT=cand_words[:, P * t : P * (t + 1)].bitcast(FP8X4),
+                    lhsT_scale=cand_scales[:, P * t : P * (t + 1)],
+                    rhs=z_words[:].bitcast(FP8X4),
+                    rhs_scale=z_scales[:],
+                    start=True,
+                    stop=True,
+                )
+            nc.vector.tensor_scalar(s[0][:, lo:hi], first[:], 0.0625, None, MULT)
+        for t in range(1, PACK):
+            nc.vector.tensor_scalar(s[t][:], s_acc[t][:], 0.0625, None, MULT)
+
+        result = sbuf("result", [P, PACK, S], F32)
+        out_scales = sbuf("out_scales", [P, S], U8)
+        out_rows = out_0.rearrange("(p t) j -> p t j", t=PACK)
+        out_words_dram = out_1[0].rearrange("p n t -> p (n t)").bitcast(I32)
+        for c, (lo, hi) in enumerate(OUT_CHUNKS):
+            n = hi - lo
+            for t in range(PACK):
+                col = slice(t, t + 1)
+                sg = sbuf(f"sg{c}{t}", [P, n], F32)
+                nc.scalar.activation(
+                    sg[:], s[t][:].indirect(entries(n2_l, lo, hi)), SIGMOID, bias=bias1[:, col], scale=sl_c[:, col]
+                )
+                sg2 = sbuf(f"sg2{c}{t}", [P, n], F32)
+                nc.scalar.activation(
+                    sg2[:], s[t][:].indirect(entries(n3_l, lo, hi)), SIGMOID, bias=bias2[:, col], scale=scale2[:, col]
+                )
+                gated = sbuf(f"gated{c}{t}", [P, n], F32)
+                nc.vector.scalar_tensor_tensor(gated[:], s[t][:, lo:hi], 2.0, sg[:], MULT, MULT)
+                nc.vector.tensor_tensor(result[:, t, lo:hi], gated[:], sg2[:], MULT)
+                nc.sync.dma_start(out=out_rows[:, t, lo:hi], in_=result[:, t, lo:hi])
+            rounded = sbuf(f"rounded{c}", [P, PACK * n], BF16)
+            nc.vector.tensor_copy(into_words(rounded[:]), by_lines(result[:, :, lo:hi]))
+            out_words = sbuf(f"out_words{c}", [P, n], U32)
+            nc.vector.quantize_mx(out=out_words[:].bitcast(FP8X4), scales=out_scales[:, lo:hi], in_=rounded[:])
+            nc.sync.dma_start(out=out_words_dram[:, lo:hi], in_=out_words[:].bitcast(I32))
+        for q in range(4):
+            queue = nc.scalar if q % 2 == 0 else nc.sync
+            queue.dma_start(
+                out=out_2[0].bitcast(I32)[4 * q : 4 * q + 4, :], in_=out_scales[:].bitcast(I32)[32 * q : 32 * q + 4, :]
+            )

@@ -25,6 +25,8 @@ HALVES = [(0, 256), (256, 512)]
 Z_CHUNKS = [(0, 128), (128, 256), (256, 384), (384, 512)]
 OUT_CHUNKS = [(0, 256), (256, 384), (384, 512)]
 SCALAR_TILES = (0, 1)
+VECTOR_TILES = (2, 3)
+VECTOR_CHUNKS = 0
 
 
 def entries(list_tile, lo, hi):
@@ -58,59 +60,58 @@ def tile_picked_hcandtwiceecr_none_po_kernel(
             nc.sync.dma_start(list_tile[:], dram)
             return list_tile
 
-        def load_rows(columns, dram):
-            nc.sync.dma_start(out=columns, in_=dram.rearrange("(p t) o -> p (t o)", t=PACK))
+        def load_rows(queue, columns, dram):
+            queue.dma_start(out=columns, in_=dram.rearrange("(p t) o -> p (t o)", t=PACK))
             return columns
 
-        table_scales = sbuf("table_scales", [P, T], U8)
-        w_scales_raw = sbuf("w_scales_raw", [P, S], U8)
         place_scales = sbuf("place_scales", [P, S], U8)
         nc.vector.memset(place_scales[:].bitcast(I32), 0)
         cand_scales = sbuf("cand_scales", [P, S], U8)
         nc.vector.memset(cand_scales[:].bitcast(I32), 0)
 
         offs_l = load_list("offs_l", offs)
-        nc.sync.dma_start(
+        table_scales = sbuf("table_scales", [P, T], U8)
+        nc.scalar.dma_start(
             out=table_scales[:].bitcast(I32), in_=x_scales[0].bitcast(I32).unsqueeze(1).broadcast_to([16, 8, T // 4])
         )
-        w_raw = sbuf("w_raw", [P, 2 * S], U8)
-        for q in range(4):
-            queue = nc.sync if q < 2 else nc.gpsimd
+        cand_l = load_list("cand_l", cand)
+        w_scales_raw = sbuf("w_scales_raw", [P, S], U8)
+        for q, queue in enumerate((nc.scalar, nc.scalar, nc.gpsimd, nc.gpsimd)):
             queue.dma_start(
                 out=w_scales_raw[:].bitcast(I32)[32 * q : 32 * (q + 1), :],
                 in_=w1_scales[0].bitcast(I32)[4 * q : 4 * q + 4, :].unsqueeze(0).broadcast_to([8, 4, S // 4]),
             )
-        nc.sync.dma_start(out=w_raw[:].bitcast(I32), in_=w1_words[0].bitcast(I32))
-        gs_c = load_rows(sbuf("gs_c", [P, PACK], F32)[:], gs)
-        cand_l = load_list("cand_l", cand)
         table_words = sbuf("table_words", [P, T], U32)
         nc.sync.dma_start(out=table_words[:].bitcast(I32), in_=x_words[0].rearrange("p n t -> p (n t)").bitcast(I32))
-        n1_l = load_list("n1_l", n1)
-        n2_l = load_list("n2_l", n2)
-        n3_l = load_list("n3_l", n3)
+        w_raw = sbuf("w_raw", [P, 2 * S], U8)
+        nc.sync.dma_start(out=w_raw[:].bitcast(I32), in_=w1_words[0].bitcast(I32))
+        gs_c = load_rows(nc.sync, sbuf("gs_c", [P, PACK], F32)[:], gs)
 
         place_bytes = sbuf("place_bytes", [P, S], U8)
         nc.vector.tensor_copy(place_bytes[:], table_scales[:].indirect(offs_l[:]))
-        place_scale_rows((nc.scalar, nc.scalar, nc.sync, nc.sync), place_scales, place_bytes)
+        place_scale_rows((nc.scalar, nc.sync, nc.scalar, nc.sync), place_scales, place_bytes)
+        w_scales = sbuf("w_scales", [P, S], U8)
+        nc.vector.tensor_copy(
+            w_scales[:].rearrange("p (t m) -> p t m", t=PACK), w_scales_raw[:].rearrange("p (m t) -> p t m", t=PACK)
+        )
+        n1_l = load_list("n1_l", n1)
+        n2_l = load_list("n2_l", n2)
+        n3_l = load_list("n3_l", n3)
 
         w_words = sbuf("w_words", [P, 2 * S], U8)
         nc.scalar.copy(
             w_words[:].bitcast(U16).rearrange("p (t m) -> p t m", t=PACK),
             w_raw[:].bitcast(U16).rearrange("p (m t) -> p t m", t=PACK),
         )
-        w_scales = sbuf("w_scales", [P, S], U8)
-        nc.vector.tensor_copy(
-            w_scales[:].rearrange("p (t m) -> p t m", t=PACK), w_scales_raw[:].rearrange("p (m t) -> p t m", t=PACK)
-        )
 
         gate_rows = held.tile([P, 4, 8], F32, name="gate_rows", tag="w_scales_raw", align_bytes=64)
-        sl_c, th_c, sl2_c, th2_c = [load_rows(gate_rows[:, v, 0:PACK], dram) for v, dram in enumerate((sl, th, sl2, th2))]
+        sl_c, th_c, sl2_c, th2_c = [load_rows(nc.sync, gate_rows[:, v, 0:PACK], dram) for v, dram in enumerate((sl, th, sl2, th2))]
 
         place_words = sbuf("place_words", [P, S], U32)
         y = [sbuf(f"y{t}", [P, S], F32) for t in range(PACK)]
         for h, (lo, hi) in enumerate(HALVES):
             nc.vector.tensor_copy(place_words[:, lo:hi], table_words[:].indirect(entries(offs_l, lo, hi)))
-            for t in range(PACK):
+            for t in VECTOR_TILES + SCALAR_TILES:
                 acc = psum.tile([P, hi - lo], F32, name=f"y_acc{h}{t}", tag=f"bank{PACK * h + t}")
                 nc.tensor.matmul_mx(
                     out=acc[:],
@@ -140,7 +141,7 @@ def tile_picked_hcandtwiceecr_none_po_kernel(
         )
 
         st = sbuf("st", [P, PACK, S], F32)
-        for t in (0, 2, 1, 3):
+        for t in VECTOR_TILES + SCALAR_TILES:
             y_at = sbuf(f"y_at{t}", [P, S], F32)
             for lo, hi in HALVES:
                 looked_up = y[t][:].indirect(entries(n1_l, lo, hi))
@@ -161,9 +162,16 @@ def tile_picked_hcandtwiceecr_none_po_kernel(
         s_acc = {t: psum.tile([P, S], F32, name=f"s_acc{t}", tag=f"bank{PACK + t}") for t in range(1, PACK)}
         for c, (lo, hi) in enumerate(Z_CHUNKS):
             n = hi - lo
-            half_at = sbuf(f"half_at{c}", [P, PACK, n], F32)
-            for t in (0, 2, 1, 3):
-                nc.scalar.activation(half_at[:, t, :], st[:, t, :].indirect(entries(n1_l, lo, hi)), COPY, scale=0.5)
+            half_at = held.tile([P, PACK, n], F32, name=f"half_at{c}", tag=(f"half_at{c}", f"half_at{c}", "y_at1", "y1")[c], align_bytes=64)
+            on_vector = SCALAR_TILES if c < VECTOR_CHUNKS else ()
+            for t in VECTOR_TILES + SCALAR_TILES:
+                if t not in on_vector:
+                    nc.scalar.activation(half_at[:, t, :], st[:, t, :].indirect(entries(n1_l, lo, hi)), COPY, scale=0.5)
+            if on_vector:
+                st_at = sbuf(f"st_at{c}", [P, 2, n], F32)
+                for t in on_vector:
+                    nc.vector.tensor_copy(st_at[:, t, :], st[:, t, :].indirect(entries(n1_l, lo, hi)))
+                nc.vector.tensor_scalar(half_at[:, 0:2, :], st_at[:], 0.5, None, MULT)
             z = sbuf(f"z{c}", [P, PACK * n], BF16)
             nc.vector.tensor_tensor(into_words(z[:]), by_lines(st[:, :, lo:hi]), by_lines(half_at[:]), SUBTRACT)
             z_words = sbuf(f"z_words{c}", [P, n], U32)

@@ -87,6 +87,11 @@ def tile_picked_hcandtwiceecr_none_po_kernel(
         nc.sync.dma_start(out=w_raw[:].bitcast(I32), in_=w1_words[0].bitcast(I32))
         gs_c = load_rows(nc.sync, sbuf("gs_c", [P, PACK], F32)[:], gs)
 
+        idle_in = sbuf("idle_in", [P, 1], F32)
+        nc.vector.memset(idle_in[:], 0.0)
+        idle_out = sbuf("idle_out", [P, 1], F32)
+        nc.scalar.activation(idle_out[:], idle_in[:], SIGMOID)
+
         place_bytes = sbuf("place_bytes", [P, S], U8)
         nc.vector.tensor_copy(place_bytes[:], table_scales[:].indirect(offs_l[:]))
         place_scale_rows((nc.scalar, nc.sync, nc.scalar, nc.sync), place_scales, place_bytes)

import concourse.mybir as mybir

F32 = mybir.dt.float32
BF16 = mybir.dt.bfloat16
I32 = mybir.dt.int32
U32 = mybir.dt.uint32
U16 = mybir.dt.uint16
U8 = mybir.dt.uint8
FP8X4 = mybir.dt.float8_e4m3fn_x4
FP4X4 = mybir.dt.float4_e2m1fn_x4
MULT = mybir.AluOpType.mult
ADD = mybir.AluOpType.add
SUBTRACT = mybir.AluOpType.subtract
COPY = mybir.ActivationFunctionType.Copy
SIGMOID = mybir.ActivationFunctionType.Sigmoid

P = 128
PACK = 4
T = 2048
S = 512
PER_COLUMN = 16
FLOPS = 2 * 2 * 512 * 512 * 512

HALVES = [(0, 256), (256, 512)]
Z_CHUNKS = [(0, 128), (128, 256), (256, 384), (384, 512)]
OUT_CHUNKS = [(0, 256), (256, 384), (384, 512)]
SCALAR_TILES = (0, 1)
VECTOR_TILES = (2, 3)
VECTOR_CHUNKS = 0


def entries(list_tile, lo, hi):
    return list_tile[:, lo // PER_COLUMN : hi // PER_COLUMN]


def by_lines(planes):
    return planes.rearrange("p t (c i) -> p c t i", i=4)


def into_words(values):
    return values.rearrange("p (c i t) -> p c t i", i=4, t=PACK)


def place_scale_rows(queues, placed, gathered):
    for i, queue in enumerate(queues):
        queue.dma_start(out=placed[:].bitcast(I32)[i:P:32, :], in_=gathered[:].bitcast(I32)[8 * i : P : 32, :])


def tile_picked_hcandtwiceecr_none_po_kernel(
    tc, x_words, x_scales, w1_words, w1_scales, gs, sl, th, sl2, th2, offs, n1, cand, n2, n3, out_0, out_1, out_2
):
    nc = tc.nc
    with tc.tile_pool(name="held", bufs=1) as held, tc.psum_pool(name="psum", bufs=1) as psum:

        def sbuf(name, shape, dtype):
            return held.tile(shape, dtype, name=name, align_bytes=64)

        def load_list(name, dram):
            list_tile = sbuf(name, [P, S // PER_COLUMN], U16)
            nc.sync.dma_start(list_tile[:], dram)
            return list_tile

        def load_rows(queue, columns, dram):
            queue.dma_start(out=columns, in_=dram.rearrange("(p t) o -> p (t o)", t=PACK))
            return columns

        place_scales = sbuf("place_scales", [P, S], U8)
        nc.vector.memset(place_scales[:].bitcast(I32), 0)
        cand_scales = sbuf("cand_scales", [P, S], U8)
        nc.vector.memset(cand_scales[:].bitcast(I32), 0)

        offs_l = load_list("offs_l", offs)
        table_scales = sbuf("table_scales", [P, T], U8)
        nc.scalar.dma_start(
            out=table_scales[:].bitcast(I32), in_=x_scales[0].bitcast(I32).unsqueeze(1).broadcast_to([16, 8, T // 4])
        )
        cand_l = load_list("cand_l", cand)
        w_scales_raw = sbuf("w_scales_raw", [P, S], U8)
        for q, queue in enumerate((nc.scalar, nc.scalar, nc.gpsimd, nc.gpsimd)):
            queue.dma_start(
                out=w_scales_raw[:].bitcast(I32)[32 * q : 32 * (q + 1), :],
                in_=w1_scales[0].bitcast(I32)[4 * q : 4 * q + 4, :].unsqueeze(0).broadcast_to([8, 4, S // 4]),
            )
        table_words = sbuf("table_words", [P, T], U32)
        nc.sync.dma_start(out=table_words[:].bitcast(I32), in_=x_words[0].rearrange("p n t -> p (n t)").bitcast(I32))
        w_raw = sbuf("w_raw", [P, 2 * S], U8)
        nc.sync.dma_start(out=w_raw[:].bitcast(I32), in_=w1_words[0].bitcast(I32))
        gs_c = load_rows(nc.sync, sbuf("gs_c", [P, PACK], F32)[:], gs)

        idle_in = sbuf("idle_in", [P, 1], F32)
        nc.vector.memset(idle_in[:], 0.0)
        idle_out = sbuf("idle_out", [P, 1], F32)
        nc.scalar.activation(idle_out[:], idle_in[:], SIGMOID)

        place_bytes = sbuf("place_bytes", [P, S], U8)
        nc.vector.tensor_copy(place_bytes[:], table_scales[:].indirect(offs_l[:]))
        place_scale_rows((nc.scalar, nc.sync, nc.scalar, nc.sync), place_scales, place_bytes)
        w_scales = sbuf("w_scales", [P, S], U8)
        nc.vector.tensor_copy(
            w_scales[:].rearrange("p (t m) -> p t m", t=PACK), w_scales_raw[:].rearrange("p (m t) -> p t m", t=PACK)
        )
        n1_l = load_list("n1_l", n1)
        n2_l = load_list("n2_l", n2)
        n3_l = load_list("n3_l", n3)

        w_words = sbuf("w_words", [P, 2 * S], U8)
        nc.scalar.copy(
            w_words[:].bitcast(U16).rearrange("p (t m) -> p t m", t=PACK),
            w_raw[:].bitcast(U16).rearrange("p (m t) -> p t m", t=PACK),
        )

        gate_rows = held.tile([P, 4, 8], F32, name="gate_rows", tag="w_scales_raw", align_bytes=64)
        sl_c, th_c, sl2_c, th2_c = [load_rows(nc.sync, gate_rows[:, v, 0:PACK], dram) for v, dram in enumerate((sl, th, sl2, th2))]

        place_words = sbuf("place_words", [P, S], U32)
        y = [sbuf(f"y{t}", [P, S], F32) for t in range(PACK)]
        for h, (lo, hi) in enumerate(HALVES):
            nc.vector.tensor_copy(place_words[:, lo:hi], table_words[:].indirect(entries(offs_l, lo, hi)))
            for t in VECTOR_TILES + SCALAR_TILES:
                acc = psum.tile([P, hi - lo], F32, name=f"y_acc{h}{t}", tag=f"bank{PACK * h + t}")
                nc.tensor.matmul_mx(
                    out=acc[:],
                    lhsT=w_words[:, 2 * P * t : 2 * P * (t + 1)].bitcast(FP4X4),
                    lhsT_scale=w_scales[:, P * t : P * (t + 1)],
                    rhs=place_words[:, lo:hi].bitcast(FP8X4),
                    rhs_scale=place_scales[:, lo:hi],
                    start=True,
                    stop=True,
                )
                nc.scalar.activation(y[t][:, lo:hi], acc[:], COPY, scale=gs_c[:, t : t + 1])

        cand_bytes = sbuf("cand_bytes", [P, S], U8)
        nc.vector.tensor_copy(cand_bytes[:], table_scales[:].indirect(cand_l[:]))
        cand_bytes_dealt = sbuf("cand_bytes_dealt", [P, S], U8)
        nc.vector.tensor_copy(
            cand_bytes_dealt[:].rearrange("p (t m) -> p t m", t=PACK),
            cand_bytes[:].rearrange("p (m t) -> p t m", t=PACK),
        )
        place_scale_rows((nc.sync,) * 4, cand_scales, cand_bytes_dealt)
        cand_picked = sbuf("cand_picked", [P, S], U32)
        nc.vector.tensor_copy(cand_picked[:], table_words[:].indirect(cand_l[:]))
        cand_words = sbuf("cand_words", [P, S], U32)
        nc.vector.tensor_copy(
            cand_words[:].bitcast(I32).rearrange("p (t m) -> p t m", t=PACK),
            cand_picked[:].bitcast(I32).rearrange("p (m t) -> p t m", t=PACK),
        )

        st = sbuf("st", [P, PACK, S], F32)
        for t in VECTOR_TILES + SCALAR_TILES:
            y_at = sbuf(f"y_at{t}", [P, S], F32)
            for lo, hi in HALVES:
                looked_up = y[t][:].indirect(entries(n1_l, lo, hi))
                if t in SCALAR_TILES:
                    nc.scalar.activation(y_at[:, lo:hi], looked_up, COPY)
                else:
                    nc.vector.tensor_copy(y_at[:, lo:hi], looked_up)
            nc.vector.tensor_tensor(st[:, t, :], y[t][:], y_at[:], SUBTRACT)

        bias1 = sbuf("bias1", [P, PACK], F32)
        nc.vector.scalar_tensor_tensor(bias1[:], sl_c, -1.0, th_c, MULT, MULT)
        scale2 = sbuf("scale2", [P, PACK], F32)
        nc.vector.tensor_scalar(scale2[:], sl2_c, -1.0, None, MULT)
        bias2 = sbuf("bias2", [P, PACK], F32)
        nc.vector.tensor_tensor(bias2[:], sl2_c, th2_c, MULT)

        s = [sbuf(f"s{t}", [P, S], F32) for t in range(PACK)]
        s_acc = {t: psum.tile([P, S], F32, name=f"s_acc{t}", tag=f"bank{PACK + t}") for t in range(1, PACK)}
        for c, (lo, hi) in enumerate(Z_CHUNKS):
            n = hi - lo
            half_at = held.tile([P, PACK, n], F32, name=f"half_at{c}", tag=(f"half_at{c}", f"half_at{c}", "y_at1", "y1")[c], align_bytes=64)
            on_vector = SCALAR_TILES if c < VECTOR_CHUNKS else ()
            for t in VECTOR_TILES + SCALAR_TILES:
                if t not in on_vector:
                    nc.scalar.activation(half_at[:, t, :], st[:, t, :].indirect(entries(n1_l, lo, hi)), COPY, scale=0.5)
            if on_vector:
                st_at = sbuf(f"st_at{c}", [P, 2, n], F32)
                for t in on_vector:
                    nc.vector.tensor_copy(st_at[:, t, :], st[:, t, :].indirect(entries(n1_l, lo, hi)))
                nc.vector.tensor_scalar(half_at[:, 0:2, :], st_at[:], 0.5, None, MULT)
            z = sbuf(f"z{c}", [P, PACK * n], BF16)
            nc.vector.tensor_tensor(into_words(z[:]), by_lines(st[:, :, lo:hi]), by_lines(half_at[:]), SUBTRACT)
            z_words = sbuf(f"z_words{c}", [P, n], U32)
            z_scales = sbuf(f"z_scales{c}", [P, n], U8)
            nc.vector.quantize_mx(out=z_words[:].bitcast(FP8X4), scales=z_scales[:], in_=z[:])
            first = psum.tile([P, n], F32, name=f"s_first{c}", tag=f"bank{c}")
            for t in range(PACK):
                nc.tensor.matmul_mx(
                    out=first[:] if t == 0 else s_acc[t][:, lo:hi],
                    lhsT=cand_words[:, P * t : P * (t + 1)].bitcast(FP8X4),
                    lhsT_scale=cand_scales[:, P * t : P * (t + 1)],
                    rhs=z_words[:].bitcast(FP8X4),
                    rhs_scale=z_scales[:],
                    start=True,
                    stop=True,
                )
            nc.vector.tensor_scalar(s[0][:, lo:hi], first[:], 0.0625, None, MULT)
        for t in range(1, PACK):
            nc.vector.tensor_scalar(s[t][:], s_acc[t][:], 0.0625, None, MULT)

        result = sbuf("result", [P, PACK, S], F32)
        out_scales = sbuf("out_scales", [P, S], U8)
        out_rows = out_0.rearrange("(p t) j -> p t j", t=PACK)
        out_words_dram = out_1[0].rearrange("p n t -> p (n t)").bitcast(I32)
        for c, (lo, hi) in enumerate(OUT_CHUNKS):
            n = hi - lo
            for t in range(PACK):
                col = slice(t, t + 1)
                sg = sbuf(f"sg{c}{t}", [P, n], F32)
                nc.scalar.activation(
                    sg[:], s[t][:].indirect(entries(n2_l, lo, hi)), SIGMOID, bias=bias1[:, col], scale=sl_c[:, col]
                )
                sg2 = sbuf(f"sg2{c}{t}", [P, n], F32)
                nc.scalar.activation(
                    sg2[:], s[t][:].indirect(entries(n3_l, lo, hi)), SIGMOID, bias=bias2[:, col], scale=scale2[:, col]
                )
                gated = sbuf(f"gated{c}{t}", [P, n], F32)
                nc.vector.scalar_tensor_tensor(gated[:], s[t][:, lo:hi], 2.0, sg[:], MULT, MULT)
                nc.vector.tensor_tensor(result[:, t, lo:hi], gated[:], sg2[:], MULT)
                nc.sync.dma_start(out=out_rows[:, t, lo:hi], in_=result[:, t, lo:hi])
            rounded = sbuf(f"rounded{c}", [P, PACK * n], BF16)
            nc.vector.tensor_copy(into_words(rounded[:]), by_lines(result[:, :, lo:hi]))
            out_words = sbuf(f"out_words{c}", [P, n], U32)
            nc.vector.quantize_mx(out=out_words[:].bitcast(FP8X4), scales=out_scales[:, lo:hi], in_=rounded[:])
            nc.sync.dma_start(out=out_words_dram[:, lo:hi], in_=out_words[:].bitcast(I32))
        for q in range(4):
            queue = nc.scalar if q % 2 == 0 else nc.sync
            queue.dma_start(
                out=out_2[0].bitcast(I32)[4 * q : 4 * q + 4, :], in_=out_scales[:].bitcast(I32)[32 * q : 32 * q + 4, :]
            )
